import numpy as np
import ml_dtypes


def mxq(x, axis, fmt="e4m3"):
    dtype, down = {"e4m3": (ml_dtypes.float8_e4m3fn, 7), "e5m2": (ml_dtypes.float8_e5m2, 14)}[fmt]
    v = np.moveaxis(np.asarray(x, np.float32).astype(ml_dtypes.bfloat16).astype(np.float64), axis, -1)
    blocks = v.reshape(v.shape[:-1] + (-1, 32))
    amax = np.abs(blocks).max(-1, keepdims=True)
    byte = np.maximum(np.where(amax > 0, np.frexp(amax)[1] - 1 + 127, 0) - down, 1)
    scale = np.exp2(byte - 127.0)
    codes = (blocks / scale).astype(np.float32).astype(dtype).astype(np.float64)
    return np.moveaxis((codes * scale).reshape(v.shape), -1, axis)


WIDE = False


def mx_kscale(k):
    if not WIDE:
        return np.ones(k)
    levels = np.array([10, -10, 5, -5, 0])
    if k % 512:
        return np.exp2(np.random.permutation(np.resize(levels, k // 32))).repeat(32)
    a = np.empty((k // 512, 16))
    for p in range(k // 512):
        a[p, :8] = np.random.permutation(np.resize(levels, 8))
        for g in range(8):
            far = levels[np.abs(levels - a[p, g]) >= 10]
            a[p, g + 8] = far[np.random.randint(len(far))]
    return np.exp2(a.ravel()).repeat(32)


def f64(x):
    return np.asarray(x).astype(np.float64)


def striped(idx):
    return np.tile(idx.reshape(-1, 16).T, (8, 1)).astype(np.uint16)


def unstriped(offs):
    return offs[:16].T.reshape(-1).astype(np.int64)


def striped8(idx):
    return np.concatenate([x.reshape(-1, 16).T for x in idx]).astype(np.uint16)


def runs(offs, k):
    lists = np.stack([offs[16 * r : 16 * r + 16].T.reshape(-1) for r in range(8)]).astype(np.int64)
    return lists[np.arange(k) % 512 // 64]


def pack_weight(w):
    k, n = w.shape
    w = f64(np.asarray(w, np.float32).astype(ml_dtypes.bfloat16)).reshape(k // 32, 32, n)
    amax = np.abs(w).max(1)
    byte = np.clip(np.where(amax > 0, np.frexp(amax)[1] - 1 + 127 - 7, 1), 1, 254)
    scaled = (w * np.exp2(127.0 - byte)[:, None, :]).reshape(k, n).astype(np.float32)
    words = np.ascontiguousarray(scaled.reshape(k // 512, 128, 4, n).transpose(0, 1, 3, 2)).astype(ml_dtypes.float8_e4m3fn).view(np.uint8)
    return words, np.ascontiguousarray(byte.astype(np.uint8).reshape(k // 512, 16, n))


def unpack_weight(words, scales):
    g, p, n, _ = words.shape
    vals = np.ascontiguousarray(words).view(ml_dtypes.float8_e4m3fn).astype(np.float64) * np.repeat(np.exp2(scales.astype(np.float64) - 127.0), 8, axis=1)[..., None]
    return vals.transpose(0, 1, 3, 2).reshape(g * 512, n)


def sigmoid(v):
    return 1.0 / (1.0 + np.exp(-np.maximum(v, -700.0)))


K, T, S, N, H, W, J = 512, 2048, 512, 512, 512, 256, 512


def setup_inputs():
    n = np.random.standard_normal
    s = mx_kscale(K)[:, None]
    u = mx_kscale(H)
    packed_xT = pack_weight(n((K, T)) * s)
    return {
        "x_words": packed_xT[0],
        "x_scales": packed_xT[1],
        "w1": (n((K, H)) / np.sqrt(K) / s).astype(np.float32),
        "w2": (n((K, H)) / np.sqrt(K) / s).astype(np.float32),
        "w3": (n((K, H)) / np.sqrt(K) / s).astype(np.float32),
        "gn": (np.random.uniform(0.5, 1.5, (H, 1)) * u[:, None]).astype(np.float32),
        "w4": (n((H, N)) / np.sqrt(H) / u[:, None]).astype(np.float32),
        "tab": n((N, J)).astype(np.float32),
        "offs": striped(np.random.permutation(T)[:S]),
        "two": striped(np.random.permutation(T)[:S]),
        "three": striped(np.random.permutation(T)[:S]),
        "n1": striped8(np.stack([np.random.permutation(S)[:W] for _ in range(8)])),
        "n2": striped8(np.stack([np.random.permutation(S)[:W] for _ in range(8)])),
        "n3": striped8(np.stack([np.random.permutation(S) for _ in range(8)])),
        "n4": striped8(np.stack([np.random.permutation(S) for _ in range(8)])),
        "n5": striped8(np.random.randint(0, J, (8, S))),
        "n6": striped8(np.stack([np.random.permutation(S) for _ in range(8)])),
    }


def reference(x_words, x_scales, w1, w2, w3, gn, w4, tab, offs, two, three, n1, n2, n3, n4, n5, n6):
    x_two = unpack_weight(x_words, x_scales)[:, unstriped(two)]
    d = mxq(f64(w2), 0, "e4m3").T @ x_two
    xq = unpack_weight(x_words, x_scales)[:, unstriped(offs)]
    y = mxq(f64(w1), 0, "e4m3").T @ xq
    ra = d[np.arange(H)[:, None], runs(n2, H)] - (0.5 * (y[np.arange(H)[:, None], runs(n1, H)]))
    m1 = y.copy()
    m1[np.arange(H)[:, None], runs(n1, H)] = ra
    x_three = unpack_weight(x_words, x_scales)[:, unstriped(three)]
    b = mxq(f64(w3), 0, "e4m3").T @ x_three
    z = f64(gn) * (m1 * (sigmoid(b[np.arange(H)[:, None], runs(n4, H)])) - (0.5 * (m1[np.arange(H)[:, None], runs(n3, H)])))
    h = mxq(f64(w4), 0, "e4m3").T @ mxq(z, 0, "e4m3")
    return np.maximum(h + f64(tab)[np.arange(N)[:, None], runs(n5, N)], h[np.arange(N)[:, None], runs(n6, N)])

@@ -1,0 +1,245 @@
+from contextlib import ExitStack
+
+import concourse.mybir as mybir
+
+K, T, S, N, H, W, J = 512, 2048, 512, 512, 512, 256, 512
+FLOPS = 2 * K * H * S * 3 + 2 * H * N * S
+
+F32 = mybir.dt.float32
+BF16 = mybir.dt.bfloat16
+I32 = mybir.dt.int32
+U32 = mybir.dt.uint32
+U16 = mybir.dt.uint16
+U8 = mybir.dt.uint8
+FP8X4 = mybir.dt.float8_e4m3fn_x4
+MULT = mybir.AluOpType.mult
+ADD = mybir.AluOpType.add
+SUBTRACT = mybir.AluOpType.subtract
+MAX = mybir.AluOpType.max
+COPY = mybir.ActivationFunctionType.Copy
+SIGMOID = mybir.ActivationFunctionType.Sigmoid
+
+P = 128
+PACK = 4
+TILES = 4
+HALVES = 2
+HALF = S // HALVES
+LIST_ROWS = 16
+
+
+def tile_picked_trioputbgatebkind_none_p_kernel(
+    tc, x_words, x_scales, w1, w2, w3, gn, w4, tab, offs, two, three, n1, n2, n3, n4, n5, n6, out
+):
+    nc = tc.nc
+    with ExitStack() as ctx:
+        keep = ctx.enter_context(tc.tile_pool(name="keep", bufs=1))
+        psum = ctx.enter_context(tc.psum_pool(name="psum", bufs=8))
+
+        def load_list(name, src):
+            tile = keep.tile(list(src.shape), U16, name=name)
+            nc.sync.dma_start(tile[:], src)
+            return tile
+
+        def load_weight(name, src):
+            tile = keep.tile([P, PACK, H], F32, name=name)
+            nc.sync.dma_start(tile[:], src.rearrange("(p j) c -> p j c", j=PACK))
+            return tile
+
+        def dealt_rows(src, t):
+            return src.rearrange("(b t q) c -> t b q c", t=TILES, q=8)[t]
+
+        def half_of(lst, half):
+            cols = HALF // LIST_ROWS
+            return lst[:, half * cols : (half + 1) * cols]
+
+        x_bytes = keep.tile([P, T], U8, name="x_bytes")
+        for quad in range(4):
+            rows = x_scales[0, 4 * quad : 4 * quad + 4, :].bitcast(I32)
+            nc.sync.dma_start(
+                x_bytes[32 * quad : 32 * quad + 32, :].bitcast(I32),
+                rows.unsqueeze(0).broadcast_to([8, 4, T // 4]),
+            )
+
+        offs_sb = load_list("offs_sb", offs)
+        two_sb = load_list("two_sb", two)
+        three_sb = load_list("three_sb", three)
+        x_codes = keep.tile([P, T], I32, name="x_codes")
+        nc.sync.dma_start(x_codes[:], x_words[0].rearrange("p c r -> p (c r)").bitcast(I32))
+        w1_raw = load_weight("w1_raw", w1)
+        w2_raw = load_weight("w2_raw", w2)
+        gain = []
+        for t in range(TILES):
+            gain_t = keep.tile([P, 1], F32, name=f"gain{t}")
+            nc.sync.dma_start(gain_t[:], dealt_rows(gn, t))
+            gain.append(gain_t)
+        n1_sb = load_list("n1_sb", n1)
+        n2_sb = load_list("n2_sb", n2)
+        w3_raw = load_weight("w3_raw", w3)
+        n4_sb = load_list("n4_sb", n4)
+        n3_sb = load_list("n3_sb", n3)
+        w4_raw = keep.tile([P, PACK, N], F32, name="w4_raw")
+        for j in range(PACK):
+            nc.sync.dma_start(w4_raw[:, j, :], dealt_rows(w4, j))
+        n5_sb = load_list("n5_sb", n5)
+        n6_sb = load_list("n6_sb", n6)
+        tab_sb = []
+        for t in range(TILES):
+            tab_t = keep.tile([P, J], F32, name=f"tab{t}")
+            nc.sync.dma_start(tab_t[:], dealt_rows(tab, t))
+            tab_sb.append(tab_t)
+
+        def pick_words(name, lst):
+            picked = keep.tile([P, S], U32, name=name, align_bytes=64)
+            nc.vector.tensor_copy(picked[:], x_codes[:].bitcast(U32).indirect(lst[:]))
+            return picked
+
+        def pick_bytes(name, lst):
+            picked = keep.tile([P, S], U8, name=name, align_bytes=64)
+            nc.vector.tensor_copy(picked[:], x_bytes[:].indirect(lst[:]))
+            return picked
+
+        def quantise_weight_tile(name, raw, t):
+            grouped = keep.tile([P, P * PACK], BF16, name=f"{name}_grouped{t}", align_bytes=64)
+            nc.scalar.copy(
+                grouped[:].rearrange("p (b u i j) -> p b u j i", u=2, i=4, j=PACK),
+                raw[:].rearrange("p j (b t u i) -> p t b u j i", t=TILES, u=2, i=4)[:, t],
+            )
+            codes = keep.tile([P, P], U32, name=f"{name}_codes{t}", align_bytes=64)
+            scales = keep.tile([P, P], U8, name=f"{name}_scales{t}", align_bytes=64)
+            nc.vector.quantize_mx(out=codes[:].bitcast(FP8X4), scales=scales[:], in_=grouped[:])
+            return codes, scales
+
+        def product(weight, codes, scales, width):
+            acc = psum.tile([P, S], F32, name="acc")
+            nc.tensor.matmul_mx(
+                out=acc[:, 0:width],
+                lhsT=weight[0][:].bitcast(FP8X4),
+                lhsT_scale=weight[1][:],
+                rhs=codes[:].bitcast(FP8X4),
+                rhs_scale=scales[:],
+                start=True,
+                stop=True,
+            )
+            return acc[:, 0:width]
+
+        y_bytes = pick_bytes("y_bytes", offs_sb)
+        d_bytes = pick_bytes("d_bytes", two_sb)
+        b_bytes = pick_bytes("b_bytes", three_sb)
+        y_words = pick_words("y_words", offs_sb)
+        d_words = pick_words("d_words", two_sb)
+        b_words = pick_words("b_words", three_sb)
+        w1_mx = [quantise_weight_tile("w1", w1_raw, t) for t in range(TILES)]
+        w2_mx = [quantise_weight_tile("w2", w2_raw, t) for t in range(TILES)]
+
+        m1, own, other = [], [], []
+
+        def fetch_pair(t):
+            y_t = keep.tile([P, S], F32, name=f"m1_{t}")
+            nc.scalar.activation(y_t[:], product(w1_mx[t], y_words, y_bytes, S), COPY, scale=gain[t][:])
+            d_t = keep.tile([P, S], F32, name=f"d{t}")
+            nc.scalar.activation(d_t[:], product(w2_mx[t], d_words, d_bytes, S), COPY, scale=gain[t][:])
+            own_t = keep.tile([P, W], F32, name=f"own{t}")
+            nc.vector.tensor_scalar(own_t[:], y_t[:].indirect(n1_sb[:]), -0.5, 0.0, MULT, ADD)
+            other_t = keep.tile([P, W], F32, name=f"other{t}")
+            nc.vector.tensor_copy(other_t[:], d_t[:].indirect(n2_sb[:]))
+            m1.append(y_t)
+            own.append(own_t)
+            other.append(other_t)
+
+        def put_back(t):
+            nc.vector.tensor_tensor(m1[t][:].indirect(n1_sb[:]), own[t][:], other[t][:], ADD)
+
+        fetch_pair(0)
+        fetch_pair(1)
+        put_back(0)
+        w3_mx = [quantise_weight_tile("w3", w3_raw, t) for t in range(TILES)]
+        fetch_pair(2)
+        put_back(1)
+        fetch_pair(3)
+        put_back(2)
+        put_back(3)
+
+        def cols_of(half):
+            return slice(half * HALF, (half + 1) * HALF)
+
+        b = []
+        gate = [keep.tile([P, S], F32, name=f"gate{t}") for t in range(TILES)]
+
+        def fetch_gate(t, half):
+            nc.scalar.activation(gate[t][:, cols_of(half)], b[t][:].indirect(half_of(n4_sb, half)), SIGMOID)
+
+        for t in range(TILES):
+            b_t = keep.tile([P, S], F32, name=f"b{t}")
+            nc.scalar.copy(b_t[:], product(w3_mx[t], b_words, b_bytes, S))
+            b.append(b_t)
+            fetch_gate(t, 0)
+        for t in range(TILES):
+            fetch_gate(t, 1)
+        w4_mx = [quantise_weight_tile("w4", w4_raw, t) for t in range(TILES)]
+
+        h = [keep.tile([P, S], F32, name=f"h{t}") for t in range(TILES)]
+
+        def gate_tile(dst, t, half):
+            nc.vector.scalar_tensor_tensor(dst, m1[t][:, cols_of(half)], 2.0, gate[t][:, cols_of(half)], MULT, MULT)
+
+        def z_plane(dst, gated_t, t, half):
+            nc.vector.tensor_tensor(dst, m1[t][:].indirect(half_of(n3_sb, half)), gated_t, SUBTRACT)
+
+        def quantise_z(z_planes, half, tag):
+            z_grouped = keep.tile([P, HALF * PACK], BF16, name=f"z_grouped{half}", tag=tag, align_bytes=64)
+            nc.scalar.activation(
+                z_grouped[:].rearrange("p (c i t) -> p c t i", i=4, t=PACK),
+                z_planes[:].rearrange("p t (c i) -> p c t i", i=4),
+                COPY,
+                scale=-0.5,
+            )
+            z_codes = keep.tile([P, HALF], U32, name=f"z_codes{half}", align_bytes=64)
+            z_scales = keep.tile([P, HALF], U8, name=f"z_scales{half}", align_bytes=64)
+            nc.vector.quantize_mx(out=z_codes[:].bitcast(FP8X4), scales=z_scales[:], in_=z_grouped[:])
+            for t in range(TILES):
+                nc.scalar.copy(h[t][:, cols_of(half)], product(w4_mx[t], z_codes, z_scales, HALF))
+
+        def finish(first_t, second, t, half):
+            res = keep.tile([P, HALF], F32, name=f"res{t}_{half}")
+            nc.vector.tensor_tensor(res[:], first_t[:], second[:], MAX)
+            nc.sync.dma_start(dealt_rows(out, t)[:, :, cols_of(half)], res[:])
+
+        gated_a = keep.tile([P, TILES, HALF], F32, name="gated_a", tag="shared_a")
+        z_a = keep.tile([P, PACK, HALF], F32, name="z_a")
+        for t in range(TILES + 1):
+            if t < TILES:
+                gate_tile(gated_a[:, t, :], t, 0)
+            if t > 0:
+                z_plane(z_a[:, t - 1, :], gated_a[:, t - 1, :], t - 1, 0)
+        quantise_z(z_a, 0, "shared_b")
+        z_b = keep.tile([P, PACK, HALF], F32, name="z_b", tag="shared_a")
+        gated_b01 = keep.tile([P, 2, HALF], F32, name="gated_b01")
+        gated_b23 = keep.tile([P, 2, HALF], F32, name="gated_b23", tag="shared_b", align_bytes=64)
+        for pair, gated_b in enumerate((gated_b01, gated_b23)):
+            for e in range(2):
+                gate_tile(gated_b[:, e, :], 2 * pair + e, 1)
+            for e in range(2):
+                z_plane(z_b[:, 2 * pair + e, :], gated_b[:, e, :], 2 * pair + e, 1)
+        quantise_z(z_b, 1, "shared_c")
+
+        first_a = []
+        for t in range(TILES):
+            tag = "shared_c" if t == TILES - 1 else f"first_a{t}"
+            first_t = keep.tile([P, HALF], F32, name=f"first_a{t}", tag=tag, align_bytes=64)
+            nc.vector.tensor_tensor(first_t[:], tab_sb[t][:].indirect(half_of(n5_sb, 0)), h[t][:, cols_of(0)], ADD)
+            first_a.append(first_t)
+
+        waiting = None
+        for t in range(TILES):
+            for half in range(HALVES):
+                if half == 0:
+                    first_t = first_a[t]
+                else:
+                    first_t = keep.tile([P, HALF], F32, name=f"first_b{t}")
+                    nc.vector.tensor_tensor(first_t[:], tab_sb[t][:].indirect(half_of(n5_sb, 1)), h[t][:, cols_of(1)], ADD)
+                second = keep.tile([P, HALF], F32, name=f"second{t}_{half}")
+                nc.vector.tensor_copy(second[:], h[t][:].indirect(half_of(n6_sb, half)))
+                if waiting is not None:
+                    finish(*waiting)
+                waiting = (first_t, second, t, half)
+        finish(*waiting)

@@ -33,7 +33,7 @@ def tile_picked_trioputbgatebkind_none_p_kernel(
     nc = tc.nc
     with ExitStack() as ctx:
         keep = ctx.enter_context(tc.tile_pool(name="keep", bufs=1))
-        psum = ctx.enter_context(tc.psum_pool(name="psum", bufs=8))
+        psum = ctx.enter_context(tc.psum_pool(name="psum", bufs=1))
 
         def load_list(name, src):
             tile = keep.tile(list(src.shape), U16, name=name)
@@ -63,9 +63,9 @@ def tile_picked_trioputbgatebkind_none_p_kernel(
         offs_sb = load_list("offs_sb", offs)
         two_sb = load_list("two_sb", two)
         three_sb = load_list("three_sb", three)
+        w1_raw = load_weight("w1_raw", w1)
         x_codes = keep.tile([P, T], I32, name="x_codes")
         nc.sync.dma_start(x_codes[:], x_words[0].rearrange("p c r -> p (c r)").bitcast(I32))
-        w1_raw = load_weight("w1_raw", w1)
         w2_raw = load_weight("w2_raw", w2)
         gain = []
         for t in range(TILES):
@@ -98,23 +98,27 @@ def tile_picked_trioputbgatebkind_none_p_kernel(
             nc.vector.tensor_copy(picked[:], x_bytes[:].indirect(lst[:]))
             return picked
 
-        def quantise_weight_tile(name, raw, t):
-            grouped = keep.tile([P, P * PACK], BF16, name=f"{name}_grouped{t}", align_bytes=64)
-            nc.scalar.copy(
-                grouped[:].rearrange("p (b u i j) -> p b u j i", u=2, i=4, j=PACK),
-                raw[:].rearrange("p j (b t u i) -> p t b u j i", t=TILES, u=2, i=4)[:, t],
+        def quantise_weight(name, raw, tiles):
+            count = len(tiles)
+            grouped = keep.tile([P, count, P * PACK], BF16, name="grouped", tag=f"{name}_grouped{tiles[0]}", align_bytes=64)
+            for e, t in enumerate(tiles):
+                nc.scalar.copy(
+                    grouped[:, e, :].rearrange("p (b u i j) -> p b u j i", u=2, i=4, j=PACK),
+                    raw[:].rearrange("p j (b t u i) -> p t b u j i", t=TILES, u=2, i=4)[:, t],
+                )
+            codes = keep.tile([P, count * P], U32, name=f"{name}_codes{tiles[0]}", align_bytes=64)
+            scales = keep.tile([P, count * P], U8, name=f"{name}_scales{tiles[0]}", align_bytes=64)
+            nc.vector.quantize_mx(
+                out=codes[:].bitcast(FP8X4), scales=scales[:], in_=grouped[:].rearrange("p e c -> p (e c)")
             )
-            codes = keep.tile([P, P], U32, name=f"{name}_codes{t}", align_bytes=64)
-            scales = keep.tile([P, P], U8, name=f"{name}_scales{t}", align_bytes=64)
-            nc.vector.quantize_mx(out=codes[:].bitcast(FP8X4), scales=scales[:], in_=grouped[:])
-            return codes, scales
+            return [(codes[:, e * P : (e + 1) * P], scales[:, e * P : (e + 1) * P]) for e in range(count)]
 
-        def product(weight, codes, scales, width):
-            acc = psum.tile([P, S], F32, name="acc")
+        def product(weight, codes, scales, width, bank):
+            acc = psum.tile([P, S], F32, name="acc", tag=f"bank{bank}")
             nc.tensor.matmul_mx(
                 out=acc[:, 0:width],
-                lhsT=weight[0][:].bitcast(FP8X4),
-                lhsT_scale=weight[1][:],
+                lhsT=weight[0].bitcast(FP8X4),
+                lhsT_scale=weight[1],
                 rhs=codes[:].bitcast(FP8X4),
                 rhs_scale=scales[:],
                 start=True,
@@ -125,39 +129,38 @@ def tile_picked_trioputbgatebkind_none_p_kernel(
         y_bytes = pick_bytes("y_bytes", offs_sb)
         d_bytes = pick_bytes("d_bytes", two_sb)
         b_bytes = pick_bytes("b_bytes", three_sb)
+        w1_mx = [quantise_weight("w1", w1_raw, [t])[0] for t in range(TILES)]
         y_words = pick_words("y_words", offs_sb)
         d_words = pick_words("d_words", two_sb)
         b_words = pick_words("b_words", three_sb)
-        w1_mx = [quantise_weight_tile("w1", w1_raw, t) for t in range(TILES)]
-        w2_mx = [quantise_weight_tile("w2", w2_raw, t) for t in range(TILES)]
 
         m1, own, other = [], [], []
 
-        def fetch_pair(t):
-            y_t = keep.tile([P, S], F32, name=f"m1_{t}")
-            nc.scalar.activation(y_t[:], product(w1_mx[t], y_words, y_bytes, S), COPY, scale=gain[t][:])
-            d_t = keep.tile([P, S], F32, name=f"d{t}")
-            nc.scalar.activation(d_t[:], product(w2_mx[t], d_words, d_bytes, S), COPY, scale=gain[t][:])
+        def fetch_own(t, tag):
+            y_t = keep.tile([P, S], F32, name="m1", tag=tag, align_bytes=64)
+            nc.scalar.activation(y_t[:], product(w1_mx[t], y_words, y_bytes, S, t), COPY, scale=gain[t][:])
+            m1.append(y_t)
             own_t = keep.tile([P, W], F32, name=f"own{t}")
             nc.vector.tensor_scalar(own_t[:], y_t[:].indirect(n1_sb[:]), -0.5, 0.0, MULT, ADD)
+            own.append(own_t)
+
+        def fetch_other(t):
+            d_t = keep.tile([P, S], F32, name=f"d{t}")
+            nc.scalar.activation(d_t[:], product(w2_mx[t], d_words, d_bytes, S, 4 + t), COPY, scale=gain[t][:])
             other_t = keep.tile([P, W], F32, name=f"other{t}")
             nc.vector.tensor_copy(other_t[:], d_t[:].indirect(n2_sb[:]))
-            m1.append(y_t)
-            own.append(own_t)
-            other.append(other_t)
+            nc.vector.tensor_tensor(m1[t][:].indirect(n1_sb[:]), own[t][:], other_t[:], ADD)
 
-        def put_back(t):
-            nc.vector.tensor_tensor(m1[t][:].indirect(n1_sb[:]), own[t][:], other[t][:], ADD)
-
-        fetch_pair(0)
-        fetch_pair(1)
-        put_back(0)
-        w3_mx = [quantise_weight_tile("w3", w3_raw, t) for t in range(TILES)]
-        fetch_pair(2)
-        put_back(1)
-        fetch_pair(3)
-        put_back(2)
-        put_back(3)
+        fetch_own(0, "m1_0")
+        w2_mx = [quantise_weight("w2", w2_raw, [t])[0] for t in range(TILES)]
+        fetch_own(1, "w2_grouped0")
+        fetch_other(0)
+        w3_mx = quantise_weight("w3", w3_raw, range(TILES))
+        fetch_other(1)
+        for t in range(2, TILES):
+            fetch_own(t, f"w2_grouped{t}")
+            fetch_other(t)
+        w4_mx = quantise_weight("w4", w4_raw, range(TILES))
 
         def cols_of(half):
             return slice(half * HALF, (half + 1) * HALF)
@@ -170,14 +173,13 @@ def tile_picked_trioputbgatebkind_none_p_kernel(
 
         for t in range(TILES):
             b_t = keep.tile([P, S], F32, name=f"b{t}")
-            nc.scalar.copy(b_t[:], product(w3_mx[t], b_words, b_bytes, S))
+            nc.scalar.copy(b_t[:], product(w3_mx[t], b_words, b_bytes, S, t))
             b.append(b_t)
             fetch_gate(t, 0)
-        for t in range(TILES):
+        for t in range(2):
             fetch_gate(t, 1)
-        w4_mx = [quantise_weight_tile("w4", w4_raw, t) for t in range(TILES)]
 
-        h = [keep.tile([P, S], F32, name=f"h{t}") for t in range(TILES)]
+        h = [keep.tile([P, 2 * S], F32, name=f"h{t}") for t in range(TILES)]
 
         def gate_tile(dst, t, half):
             nc.vector.scalar_tensor_tensor(dst, m1[t][:, cols_of(half)], 2.0, gate[t][:, cols_of(half)], MULT, MULT)
@@ -197,11 +199,11 @@ def tile_picked_trioputbgatebkind_none_p_kernel(
             z_scales = keep.tile([P, HALF], U8, name=f"z_scales{half}", align_bytes=64)
             nc.vector.quantize_mx(out=z_codes[:].bitcast(FP8X4), scales=z_scales[:], in_=z_grouped[:])
             for t in range(TILES):
-                nc.scalar.copy(h[t][:, cols_of(half)], product(w4_mx[t], z_codes, z_scales, HALF))
+                nc.scalar.copy(h[t][:, cols_of(half)], product(w4_mx[t], z_codes, z_scales, HALF, 4 * (1 - half) + t))
 
         def finish(first_t, second, t, half):
             res = keep.tile([P, HALF], F32, name=f"res{t}_{half}")
-            nc.vector.tensor_tensor(res[:], first_t[:], second[:], MAX)
+            nc.vector.tensor_tensor(res[:], first_t, second[:, cols_of(half)], MAX)
             nc.sync.dma_start(dealt_rows(out, t)[:, :, cols_of(half)], res[:])
 
         gated_a = keep.tile([P, TILES, HALF], F32, name="gated_a", tag="shared_a")
@@ -217,29 +219,25 @@ def tile_picked_trioputbgatebkind_none_p_kernel(
         gated_b23 = keep.tile([P, 2, HALF], F32, name="gated_b23", tag="shared_b", align_bytes=64)
         for pair, gated_b in enumerate((gated_b01, gated_b23)):
             for e in range(2):
+                if pair == 1:
+                    fetch_gate(2 + e, 1)
                 gate_tile(gated_b[:, e, :], 2 * pair + e, 1)
             for e in range(2):
                 z_plane(z_b[:, 2 * pair + e, :], gated_b[:, e, :], 2 * pair + e, 1)
         quantise_z(z_b, 1, "shared_c")
 
         first_a = []
+        first_early = keep.tile([P, 2, HALF], F32, name="first_early")
+        first_late = keep.tile([P, 2, HALF], F32, name="first_late", tag="shared_c", align_bytes=64)
         for t in range(TILES):
-            tag = "shared_c" if t == TILES - 1 else f"first_a{t}"
-            first_t = keep.tile([P, HALF], F32, name=f"first_a{t}", tag=tag, align_bytes=64)
-            nc.vector.tensor_tensor(first_t[:], tab_sb[t][:].indirect(half_of(n5_sb, 0)), h[t][:, cols_of(0)], ADD)
+            first_t = (first_early if t < 2 else first_late)[:, t % 2, :]
+            nc.vector.tensor_tensor(first_t, tab_sb[t][:].indirect(half_of(n5_sb, 0)), h[t][:, cols_of(0)], ADD)
             first_a.append(first_t)
 
-        waiting = None
         for t in range(TILES):
-            for half in range(HALVES):
-                if half == 0:
-                    first_t = first_a[t]
-                else:
-                    first_t = keep.tile([P, HALF], F32, name=f"first_b{t}")
-                    nc.vector.tensor_tensor(first_t[:], tab_sb[t][:].indirect(half_of(n5_sb, 1)), h[t][:, cols_of(1)], ADD)
-                second = keep.tile([P, HALF], F32, name=f"second{t}_{half}")
-                nc.vector.tensor_copy(second[:], h[t][:].indirect(half_of(n6_sb, half)))
-                if waiting is not None:
-                    finish(*waiting)
-                waiting = (first_t, second, t, half)
-        finish(*waiting)
+            second = keep.tile([P, S], F32, name=f"second{t}")
+            nc.vector.tensor_copy(second[:], h[t][:].indirect(n6_sb[:]))
+            first_b = keep.tile([P, HALF], F32, name=f"first_b{t}")
+            nc.vector.tensor_tensor(first_b[:], tab_sb[t][:].indirect(half_of(n5_sb, 1)), h[t][:, cols_of(1)], ADD)
+            finish(first_a[t], second, t, 0)
+            finish(first_b[:], second, t, 1)

@@ -25,6 +25,7 @@ TILES = 4
 HALVES = 2
 HALF = S // HALVES
 LIST_ROWS = 16
+ROW_BYTES = 4 * S
 
 
 def tile_picked_trioputbgatebkind_none_p_kernel(
@@ -33,6 +34,7 @@ def tile_picked_trioputbgatebkind_none_p_kernel(
     nc = tc.nc
     with ExitStack() as ctx:
         keep = ctx.enter_context(tc.tile_pool(name="keep", bufs=1))
+        reused = ctx.enter_context(tc.tile_pool(name="reused", bufs=1))
         psum = ctx.enter_context(tc.psum_pool(name="psum", bufs=1))
 
         def load_list(name, src):
@@ -74,10 +76,11 @@ def tile_picked_trioputbgatebkind_none_p_kernel(
             gain.append(gain_t)
         n1_sb = load_list("n1_sb", n1)
         n2_sb = load_list("n2_sb", n2)
-        w3_raw = load_weight("w3_raw", w3)
+        w3_raw = reused.tile([P, PACK, H], F32, name="w3_raw", offset=0)
+        nc.sync.dma_start(w3_raw[:], w3.rearrange("(p j) c -> p j c", j=PACK))
         n4_sb = load_list("n4_sb", n4)
         n3_sb = load_list("n3_sb", n3)
-        w4_raw = keep.tile([P, PACK, N], F32, name="w4_raw")
+        w4_raw = reused.tile([P, PACK, N], F32, name="w4_raw", offset=TILES * ROW_BYTES)
         for j in range(PACK):
             nc.sync.dma_start(w4_raw[:, j, :], dealt_rows(w4, j))
         n5_sb = load_list("n5_sb", n5)
@@ -136,30 +139,32 @@ def tile_picked_trioputbgatebkind_none_p_kernel(
 
         m1, own, other = [], [], []
 
-        def fetch_own(t, tag):
-            y_t = keep.tile([P, S], F32, name="m1", tag=tag, align_bytes=64)
+        def fetch_own(t, y_t):
             nc.scalar.activation(y_t[:], product(w1_mx[t], y_words, y_bytes, S, t), COPY, scale=gain[t][:])
             m1.append(y_t)
             own_t = keep.tile([P, W], F32, name=f"own{t}")
             nc.vector.tensor_scalar(own_t[:], y_t[:].indirect(n1_sb[:]), -0.5, 0.0, MULT, ADD)
             own.append(own_t)
 
-        def fetch_other(t):
-            d_t = keep.tile([P, S], F32, name=f"d{t}")
+        def fetch_other(t, d_t):
             nc.scalar.activation(d_t[:], product(w2_mx[t], d_words, d_bytes, S, 4 + t), COPY, scale=gain[t][:])
             other_t = keep.tile([P, W], F32, name=f"other{t}")
             nc.vector.tensor_copy(other_t[:], d_t[:].indirect(n2_sb[:]))
             nc.vector.tensor_tensor(m1[t][:].indirect(n1_sb[:]), own[t][:], other_t[:], ADD)
 
-        fetch_own(0, "m1_0")
+        def over_w3(name, slot):
+            return reused.tile([P, S], F32, name=name, offset=slot * ROW_BYTES)
+
+        fetch_own(0, keep.tile([P, S], F32, name="m1_0"))
         w2_mx = [quantise_weight("w2", w2_raw, [t])[0] for t in range(TILES)]
-        fetch_own(1, "w2_grouped0")
-        fetch_other(0)
+        fetch_own(1, keep.tile([P, S], F32, name="m1_1", tag="w2_grouped0", align_bytes=64))
+        fetch_other(0, keep.tile([P, S], F32, name="d0"))
         w3_mx = quantise_weight("w3", w3_raw, range(TILES))
-        fetch_other(1)
-        for t in range(2, TILES):
-            fetch_own(t, f"w2_grouped{t}")
-            fetch_other(t)
+        fetch_other(1, over_w3("d1", 0))
+        fetch_own(2, over_w3("m1_2", 1))
+        fetch_other(2, over_w3("d2", 2))
+        fetch_own(3, over_w3("m1_3", 3))
+        fetch_other(3, keep.tile([P, S], F32, name="d3", tag="w3_grouped0", align_bytes=64))
         w4_mx = quantise_weight("w4", w4_raw, range(TILES))
 
         def cols_of(half):
@@ -172,7 +177,7 @@ def tile_picked_trioputbgatebkind_none_p_kernel(
             nc.scalar.activation(gate[t][:, cols_of(half)], b[t][:].indirect(half_of(n4_sb, half)), SIGMOID)
 
         for t in range(TILES):
-            b_t = keep.tile([P, S], F32, name=f"b{t}")
+            b_t = reused.tile([P, S], F32, name=f"b{t}", offset=(TILES + t) * ROW_BYTES)
             nc.scalar.copy(b_t[:], product(w3_mx[t], b_words, b_bytes, S, t))
             b.append(b_t)
             fetch_gate(t, 0)

@@ -3,7 +3,7 @@ from contextlib import ExitStack
 import concourse.mybir as mybir
 
 K, T, S, N, H, W, J = 512, 2048, 512, 512, 512, 256, 512
-FLOPS = 2 * K * H * S * 3 + 2 * H * N * S
+FLOPS = 3 * 2 * K * H * S + 2 * H * N * S
 
 F32 = mybir.dt.float32
 BF16 = mybir.dt.bfloat16
@@ -22,10 +22,17 @@ SIGMOID = mybir.ActivationFunctionType.Sigmoid
 P = 128
 PACK = 4
 TILES = 4
-HALVES = 2
-HALF = S // HALVES
+BLOCK_PARTITIONS = 8
+QUADRANT = 32
+LINE = 4
+HALF = S // 2
 LIST_ROWS = 16
+ALIGN = 64
+
 ROW_BYTES = 4 * S
+W3_AT = 0
+W4_AT = TILES * ROW_BYTES
+GAINS_AT = 2 * TILES * ROW_BYTES
 
 
 def tile_picked_trioputbgatebkind_none_p_kernel(
@@ -37,50 +44,53 @@ def tile_picked_trioputbgatebkind_none_p_kernel(
         reused = ctx.enter_context(tc.tile_pool(name="reused", bufs=1))
         psum = ctx.enter_context(tc.psum_pool(name="psum", bufs=1))
 
-        def load_list(name, src):
-            tile = keep.tile(list(src.shape), U16, name=name)
-            nc.sync.dma_start(tile[:], src)
-            return tile
-
-        def load_weight(name, src):
-            tile = keep.tile([P, PACK, H], F32, name=name)
-            nc.sync.dma_start(tile[:], src.rearrange("(p j) c -> p j c", j=PACK))
-            return tile
-
         def dealt_rows(src, t):
-            return src.rearrange("(b t q) c -> t b q c", t=TILES, q=8)[t]
+            return src.rearrange("(b t q) c -> t b q c", t=TILES, q=BLOCK_PARTITIONS)[t]
+
+        def cols_of(half):
+            return slice(half * HALF, (half + 1) * HALF)
 
         def half_of(lst, half):
-            cols = HALF // LIST_ROWS
-            return lst[:, half * cols : (half + 1) * cols]
+            return lst[:, half * HALF // LIST_ROWS : (half + 1) * HALF // LIST_ROWS]
+
+        def load_list(name, src):
+            lst = keep.tile(list(src.shape), U16, name=name)
+            nc.sync.dma_start(lst[:], src)
+            return lst
+
+        def load_first_weight(raw, src):
+            nc.sync.dma_start(raw[:], src.rearrange("(p j) c -> p j c", j=PACK))
+            return raw
+
+        warm = keep.tile([P, 2], F32, name="warm")
+        nc.gpsimd.memset(warm[:, 0:1], 0.0)
+        nc.scalar.activation(warm[:, 1:2], warm[:, 0:1], SIGMOID)
 
         x_bytes = keep.tile([P, T], U8, name="x_bytes")
-        for quad in range(4):
-            rows = x_scales[0, 4 * quad : 4 * quad + 4, :].bitcast(I32)
+        for quad in range(P // QUADRANT):
+            rows = x_scales[0, PACK * quad : PACK * (quad + 1), :].bitcast(I32)
             nc.sync.dma_start(
-                x_bytes[32 * quad : 32 * quad + 32, :].bitcast(I32),
-                rows.unsqueeze(0).broadcast_to([8, 4, T // 4]),
+                x_bytes[QUADRANT * quad : QUADRANT * (quad + 1), :].bitcast(I32),
+                rows.unsqueeze(0).broadcast_to([QUADRANT // PACK, PACK, T // 4]),
             )
-
         offs_sb = load_list("offs_sb", offs)
         two_sb = load_list("two_sb", two)
         three_sb = load_list("three_sb", three)
-        w1_raw = load_weight("w1_raw", w1)
+        w1_raw = load_first_weight(keep.tile([P, PACK, H], F32, name="w1_raw"), w1)
         x_codes = keep.tile([P, T], I32, name="x_codes")
         nc.sync.dma_start(x_codes[:], x_words[0].rearrange("p c r -> p (c r)").bitcast(I32))
-        w2_raw = load_weight("w2_raw", w2)
+        w2_raw = load_first_weight(keep.tile([P, PACK, H], F32, name="w2_raw"), w2)
         gain = []
         for t in range(TILES):
-            gain_t = keep.tile([P, 1], F32, name=f"gain{t}")
+            gain_t = reused.tile([P, 1], F32, name=f"gain{t}", offset=GAINS_AT + t * H)
             nc.sync.dma_start(gain_t[:], dealt_rows(gn, t))
             gain.append(gain_t)
         n1_sb = load_list("n1_sb", n1)
         n2_sb = load_list("n2_sb", n2)
-        w3_raw = reused.tile([P, PACK, H], F32, name="w3_raw", offset=0)
-        nc.sync.dma_start(w3_raw[:], w3.rearrange("(p j) c -> p j c", j=PACK))
+        w3_raw = load_first_weight(reused.tile([P, PACK, H], F32, name="w3_raw", offset=W3_AT), w3)
         n4_sb = load_list("n4_sb", n4)
         n3_sb = load_list("n3_sb", n3)
-        w4_raw = reused.tile([P, PACK, N], F32, name="w4_raw", offset=TILES * ROW_BYTES)
+        w4_raw = reused.tile([P, PACK, N], F32, name="w4_raw", offset=W4_AT)
         for j in range(PACK):
             nc.sync.dma_start(w4_raw[:, j, :], dealt_rows(w4, j))
         n5_sb = load_list("n5_sb", n5)
@@ -92,29 +102,37 @@ def tile_picked_trioputbgatebkind_none_p_kernel(
             tab_sb.append(tab_t)
 
         def pick_words(name, lst):
-            picked = keep.tile([P, S], U32, name=name, align_bytes=64)
+            picked = keep.tile([P, S], U32, name=name, align_bytes=ALIGN)
             nc.vector.tensor_copy(picked[:], x_codes[:].bitcast(U32).indirect(lst[:]))
             return picked
 
         def pick_bytes(name, lst):
-            picked = keep.tile([P, S], U8, name=name, align_bytes=64)
+            picked = keep.tile([P, S], U8, name=name, align_bytes=ALIGN)
             nc.vector.tensor_copy(picked[:], x_bytes[:].indirect(lst[:]))
             return picked
 
-        def quantise_weight(name, raw, tiles):
-            count = len(tiles)
-            grouped = keep.tile([P, count, P * PACK], BF16, name="grouped", tag=f"{name}_grouped{tiles[0]}", align_bytes=64)
+        def group_weight(name, raw, tiles):
+            grouped = keep.tile(
+                [P, len(tiles), P * PACK], BF16, name="grouped", tag=f"{name}_grouped{tiles[0]}", align_bytes=ALIGN
+            )
             for e, t in enumerate(tiles):
                 nc.scalar.copy(
-                    grouped[:, e, :].rearrange("p (b u i j) -> p b u j i", u=2, i=4, j=PACK),
-                    raw[:].rearrange("p j (b t u i) -> p t b u j i", t=TILES, u=2, i=4)[:, t],
+                    grouped[:, e, :].rearrange("p (b u i j) -> p b u j i", u=2, i=LINE, j=PACK),
+                    raw[:].rearrange("p j (b t u i) -> p t b u j i", t=TILES, u=2, i=LINE)[:, t],
                 )
-            codes = keep.tile([P, count * P], U32, name=f"{name}_codes{tiles[0]}", align_bytes=64)
-            scales = keep.tile([P, count * P], U8, name=f"{name}_scales{tiles[0]}", align_bytes=64)
+            return grouped
+
+        def quantise(name, grouped, scales):
+            count = grouped.shape[1]
+            codes = keep.tile([P, count * P], U32, name=f"{name}_codes", align_bytes=ALIGN)
             nc.vector.quantize_mx(
                 out=codes[:].bitcast(FP8X4), scales=scales[:], in_=grouped[:].rearrange("p e c -> p (e c)")
             )
             return [(codes[:, e * P : (e + 1) * P], scales[:, e * P : (e + 1) * P]) for e in range(count)]
+
+        def quantise_weight(name, raw, tiles):
+            scales = keep.tile([P, len(tiles) * P], U8, name=f"{name}_scales{tiles[0]}", align_bytes=ALIGN)
+            return quantise(f"{name}_{tiles[0]}", group_weight(name, raw, tiles), scales)
 
         def product(weight, codes, scales, width, bank):
             acc = psum.tile([P, S], F32, name="acc", tag=f"bank{bank}")
@@ -132,8 +150,9 @@ def tile_picked_trioputbgatebkind_none_p_kernel(
         y_bytes = pick_bytes("y_bytes", offs_sb)
         d_bytes = pick_bytes("d_bytes", two_sb)
         b_bytes = pick_bytes("b_bytes", three_sb)
-        w1_mx = [quantise_weight("w1", w1_raw, [t])[0] for t in range(TILES)]
+        w1_mx = [quantise_weight("w1", w1_raw, [t])[0] for t in range(TILES - 1)]
         y_words = pick_words("y_words", offs_sb)
+        w1_last = group_weight("w1", w1_raw, [TILES - 1])
         d_words = pick_words("d_words", two_sb)
         b_words = pick_words("b_words", three_sb)
 
@@ -147,102 +166,114 @@ def tile_picked_trioputbgatebkind_none_p_kernel(
             own.append(own_t)
 
         def fetch_other(t, d_t):
-            nc.scalar.activation(d_t[:], product(w2_mx[t], d_words, d_bytes, S, 4 + t), COPY, scale=gain[t][:])
+            nc.scalar.activation(d_t[:], product(w2_mx[t], d_words, d_bytes, S, TILES + t), COPY, scale=gain[t][:])
             other_t = keep.tile([P, W], F32, name=f"other{t}")
             nc.vector.tensor_copy(other_t[:], d_t[:].indirect(n2_sb[:]))
-            nc.vector.tensor_tensor(m1[t][:].indirect(n1_sb[:]), own[t][:], other_t[:], ADD)
+            other.append(other_t)
 
-        def over_w3(name, slot):
-            return reused.tile([P, S], F32, name=name, offset=slot * ROW_BYTES)
+        def put_back(t):
+            nc.vector.tensor_tensor(m1[t][:].indirect(n1_sb[:]), own[t][:], other[t][:], ADD)
 
-        fetch_own(0, keep.tile([P, S], F32, name="m1_0"))
-        w2_mx = [quantise_weight("w2", w2_raw, [t])[0] for t in range(TILES)]
-        fetch_own(1, keep.tile([P, S], F32, name="m1_1", tag="w2_grouped0", align_bytes=64))
+        def over_gain(name, t):
+            return reused.tile([P, H], U8, name=name, offset=GAINS_AT + t * H, align_bytes=ALIGN)
+
+        for t in range(TILES - 1):
+            fetch_own(t, keep.tile([P, S], F32, name=f"m1_{t}"))
+        w2_mx = [quantise_weight("w2", w2_raw, [t])[0] for t in range(2)]
+        w1_last_scales = keep.tile([P, P], U8, name="w1_last_scales", tag="w1_scales0", align_bytes=ALIGN)
+        w1_mx.extend(quantise("w1_last", w1_last, w1_last_scales))
+        fetch_own(3, keep.tile([P, S], F32, name="m1_3", tag="w2_grouped0", align_bytes=ALIGN))
         fetch_other(0, keep.tile([P, S], F32, name="d0"))
-        w3_mx = quantise_weight("w3", w3_raw, range(TILES))
-        fetch_other(1, over_w3("d1", 0))
-        fetch_own(2, over_w3("m1_2", 1))
-        fetch_other(2, over_w3("d2", 2))
-        fetch_own(3, over_w3("m1_3", 3))
-        fetch_other(3, keep.tile([P, S], F32, name="d3", tag="w3_grouped0", align_bytes=64))
-        w4_mx = quantise_weight("w4", w4_raw, range(TILES))
-
-        def cols_of(half):
-            return slice(half * HALF, (half + 1) * HALF)
+        put_back(0)
+        w2_mx.extend(quantise_weight("w2", w2_raw, [2, 3]))
+        fetch_other(1, keep.tile([P, S], F32, name="d1"))
+        put_back(1)
+        w3_grouped = group_weight("w3", w3_raw, range(TILES))
+        fetch_other(2, reused.tile([P, S], F32, name="d2", offset=W3_AT + 2 * ROW_BYTES))
+        w3_mx = quantise("w3", w3_grouped, over_gain("w3_scales", 2))
+        put_back(2)
+        w4_grouped = group_weight("w4", w4_raw, range(TILES))
+        fetch_other(3, reused.tile([P, S], F32, name="d3", offset=W4_AT + 3 * ROW_BYTES))
+        w4_mx = quantise("w4", w4_grouped, over_gain("w4_scales", 3))
+        put_back(3)
 
         b = []
-        gate = [keep.tile([P, S], F32, name=f"gate{t}") for t in range(TILES)]
+        gate = {}
 
-        def fetch_gate(t, half):
-            nc.scalar.activation(gate[t][:, cols_of(half)], b[t][:].indirect(half_of(n4_sb, half)), SIGMOID)
+        def fetch_gate(t, half, dst):
+            nc.scalar.activation(dst, b[t][:].indirect(half_of(n4_sb, half)), SIGMOID)
+            gate[t, half] = dst
 
+        gate_early = keep.tile([P, 2 * TILES - 1, HALF], F32, name="gate_early")
         for t in range(TILES):
-            b_t = reused.tile([P, S], F32, name=f"b{t}", offset=(TILES + t) * ROW_BYTES)
+            b_t = reused.tile([P, S], F32, name=f"b{t}", offset=W4_AT + t * ROW_BYTES)
             nc.scalar.copy(b_t[:], product(w3_mx[t], b_words, b_bytes, S, t))
             b.append(b_t)
-            fetch_gate(t, 0)
-        for t in range(2):
-            fetch_gate(t, 1)
+            fetch_gate(t, 0, gate_early[:, t, :])
+        for t in range(TILES - 1):
+            fetch_gate(t, 1, gate_early[:, TILES + t, :])
 
         h = [keep.tile([P, 2 * S], F32, name=f"h{t}") for t in range(TILES)]
 
-        def gate_tile(dst, t, half):
-            nc.vector.scalar_tensor_tensor(dst, m1[t][:, cols_of(half)], 2.0, gate[t][:, cols_of(half)], MULT, MULT)
+        def apply_gate(dst, t, half):
+            nc.vector.scalar_tensor_tensor(dst, m1[t][:, cols_of(half)], 2.0, gate[t, half], MULT, MULT)
 
-        def z_plane(dst, gated_t, t, half):
+        def make_z(dst, gated_t, t, half):
             nc.vector.tensor_tensor(dst, m1[t][:].indirect(half_of(n3_sb, half)), gated_t, SUBTRACT)
 
-        def quantise_z(z_planes, half, tag):
-            z_grouped = keep.tile([P, HALF * PACK], BF16, name=f"z_grouped{half}", tag=tag, align_bytes=64)
+        def last_layer(z_half, half):
+            z_grouped = keep.tile([P, HALF * PACK], BF16, name=f"z_grouped{half}", align_bytes=ALIGN)
             nc.scalar.activation(
-                z_grouped[:].rearrange("p (c i t) -> p c t i", i=4, t=PACK),
-                z_planes[:].rearrange("p t (c i) -> p c t i", i=4),
+                z_grouped[:].rearrange("p (c i t) -> p c t i", i=LINE, t=PACK),
+                z_half[:].rearrange("p t (c i) -> p c t i", i=LINE),
                 COPY,
                 scale=-0.5,
             )
-            z_codes = keep.tile([P, HALF], U32, name=f"z_codes{half}", align_bytes=64)
-            z_scales = keep.tile([P, HALF], U8, name=f"z_scales{half}", align_bytes=64)
+            z_codes = keep.tile([P, HALF], U32, name=f"z_codes{half}", align_bytes=ALIGN)
+            z_scales = keep.tile([P, HALF], U8, name=f"z_scales{half}", align_bytes=ALIGN)
             nc.vector.quantize_mx(out=z_codes[:].bitcast(FP8X4), scales=z_scales[:], in_=z_grouped[:])
             for t in range(TILES):
-                nc.scalar.copy(h[t][:, cols_of(half)], product(w4_mx[t], z_codes, z_scales, HALF, 4 * (1 - half) + t))
+                bank = TILES * (1 - half) + t
+                nc.scalar.copy(h[t][:, cols_of(half)], product(w4_mx[t], z_codes, z_scales, HALF, bank))
 
-        def finish(first_t, second, t, half):
-            res = keep.tile([P, HALF], F32, name=f"res{t}_{half}")
-            nc.vector.tensor_tensor(res[:], first_t, second[:, cols_of(half)], MAX)
-            nc.sync.dma_start(dealt_rows(out, t)[:, :, cols_of(half)], res[:])
-
-        gated_a = keep.tile([P, TILES, HALF], F32, name="gated_a", tag="shared_a")
-        z_a = keep.tile([P, PACK, HALF], F32, name="z_a")
+        gated_a = keep.tile([P, TILES, HALF], F32, name="gated_a", tag="half_planes")
+        z_a = keep.tile([P, TILES, HALF], F32, name="z_a")
         for t in range(TILES + 1):
             if t < TILES:
-                gate_tile(gated_a[:, t, :], t, 0)
+                apply_gate(gated_a[:, t, :], t, 0)
             if t > 0:
-                z_plane(z_a[:, t - 1, :], gated_a[:, t - 1, :], t - 1, 0)
-        quantise_z(z_a, 0, "shared_b")
-        z_b = keep.tile([P, PACK, HALF], F32, name="z_b", tag="shared_a")
-        gated_b01 = keep.tile([P, 2, HALF], F32, name="gated_b01")
-        gated_b23 = keep.tile([P, 2, HALF], F32, name="gated_b23", tag="shared_b", align_bytes=64)
-        for pair, gated_b in enumerate((gated_b01, gated_b23)):
-            for e in range(2):
-                if pair == 1:
-                    fetch_gate(2 + e, 1)
-                gate_tile(gated_b[:, e, :], 2 * pair + e, 1)
-            for e in range(2):
-                z_plane(z_b[:, 2 * pair + e, :], gated_b[:, e, :], 2 * pair + e, 1)
-        quantise_z(z_b, 1, "shared_c")
+                make_z(z_a[:, t - 1, :], gated_a[:, t - 1, :], t - 1, 0)
+        last_layer(z_a, 0)
 
-        first_a = []
+        after_z_a = keep.tile([P, 3, HALF], F32, name="after_z_a", tag="z_a")
+        fetch_gate(TILES - 1, 1, after_z_a[:, 2, :])
+        z_b = keep.tile([P, TILES, HALF], F32, name="z_b", tag="half_planes")
+        gated_b = keep.tile([P, 2, HALF], F32, name="gated_b")
+        for pair, gated_pair in enumerate((gated_b, after_z_a)):
+            for e in range(2):
+                apply_gate(gated_pair[:, e, :], 2 * pair + e, 1)
+            for e in range(2):
+                make_z(z_b[:, 2 * pair + e, :], gated_pair[:, e, :], 2 * pair + e, 1)
+        last_layer(z_b, 1)
+
+        def add_kind(dst, t, half):
+            nc.vector.tensor_tensor(dst, tab_sb[t][:].indirect(half_of(n5_sb, half)), h[t][:, cols_of(half)], ADD)
+
+        def finish(first_t, second_t, t, half):
+            res = keep.tile([P, HALF], F32, name=f"res{t}_{half}")
+            nc.vector.tensor_tensor(res[:], first_t, second_t[:, cols_of(half)], MAX)
+            nc.sync.dma_start(dealt_rows(out, t)[:, :, cols_of(half)], res[:])
+
         first_early = keep.tile([P, 2, HALF], F32, name="first_early")
-        first_late = keep.tile([P, 2, HALF], F32, name="first_late", tag="shared_c", align_bytes=64)
+        first_late = keep.tile([P, 2, HALF], F32, name="first_late", tag="half_planes")
+        first_a = [pair[:, e, :] for pair in (first_early, first_late) for e in range(2)]
         for t in range(TILES):
-            first_t = (first_early if t < 2 else first_late)[:, t % 2, :]
-            nc.vector.tensor_tensor(first_t, tab_sb[t][:].indirect(half_of(n5_sb, 0)), h[t][:, cols_of(0)], ADD)
-            first_a.append(first_t)
+            add_kind(first_a[t], t, 0)
 
         for t in range(TILES):
             second = keep.tile([P, S], F32, name=f"second{t}")
             nc.vector.tensor_copy(second[:], h[t][:].indirect(n6_sb[:]))
             first_b = keep.tile([P, HALF], F32, name=f"first_b{t}")
-            nc.vector.tensor_tensor(first_b[:], tab_sb[t][:].indirect(half_of(n5_sb, 1)), h[t][:, cols_of(1)], ADD)
+            add_kind(first_b[:], t, 1)
             finish(first_a[t], second, t, 0)
             finish(first_b[:], second, t, 1)

from contextlib import ExitStack

import concourse.mybir as mybir

K, T, S, N, H, W, J = 512, 2048, 512, 512, 512, 256, 512
FLOPS = 3 * 2 * K * H * S + 2 * H * N * S

F32 = mybir.dt.float32
BF16 = mybir.dt.bfloat16
I32 = mybir.dt.int32
U32 = mybir.dt.uint32
U16 = mybir.dt.uint16
U8 = mybir.dt.uint8
FP8X4 = mybir.dt.float8_e4m3fn_x4
MULT = mybir.AluOpType.mult
ADD = mybir.AluOpType.add
SUBTRACT = mybir.AluOpType.subtract
MAX = mybir.AluOpType.max
COPY = mybir.ActivationFunctionType.Copy
SIGMOID = mybir.ActivationFunctionType.Sigmoid

P = 128
PACK = 4
TILES = 4
BLOCK_PARTITIONS = 8
QUADRANT = 32
LINE = 4
HALF = S // 2
LIST_ROWS = 16
ALIGN = 64

ROW_BYTES = 4 * S
W3_AT = 0
W4_AT = TILES * ROW_BYTES
GAINS_AT = 2 * TILES * ROW_BYTES


def tile_picked_trioputbgatebkind_none_p_kernel(
    tc, x_words, x_scales, w1, w2, w3, gn, w4, tab, offs, two, three, n1, n2, n3, n4, n5, n6, out
):
    nc = tc.nc
    with ExitStack() as ctx:
        keep = ctx.enter_context(tc.tile_pool(name="keep", bufs=1))
        reused = ctx.enter_context(tc.tile_pool(name="reused", bufs=1))
        psum = ctx.enter_context(tc.psum_pool(name="psum", bufs=1))

        def dealt_rows(src, t):
            return src.rearrange("(b t q) c -> t b q c", t=TILES, q=BLOCK_PARTITIONS)[t]

        def cols_of(half):
            return slice(half * HALF, (half + 1) * HALF)

        def half_of(lst, half):
            return lst[:, half * HALF // LIST_ROWS : (half + 1) * HALF // LIST_ROWS]

        def load_list(name, src):
            lst = keep.tile(list(src.shape), U16, name=name)
            nc.sync.dma_start(lst[:], src)
            return lst

        def load_first_weight(raw, src):
            nc.sync.dma_start(raw[:], src.rearrange("(p j) c -> p j c", j=PACK))
            return raw

        warm = keep.tile([P, 2], F32, name="warm")
        nc.gpsimd.memset(warm[:, 0:1], 0.0)
        nc.scalar.activation(warm[:, 1:2], warm[:, 0:1], SIGMOID)

        x_bytes = keep.tile([P, T], U8, name="x_bytes")
        for quad in range(P // QUADRANT):
            rows = x_scales[0, PACK * quad : PACK * (quad + 1), :].bitcast(I32)
            nc.sync.dma_start(
                x_bytes[QUADRANT * quad : QUADRANT * (quad + 1), :].bitcast(I32),
                rows.unsqueeze(0).broadcast_to([QUADRANT // PACK, PACK, T // 4]),
            )
        offs_sb = load_list("offs_sb", offs)
        two_sb = load_list("two_sb", two)
        three_sb = load_list("three_sb", three)
        w1_raw = load_first_weight(keep.tile([P, PACK, H], F32, name="w1_raw"), w1)
        x_codes = keep.tile([P, T], I32, name="x_codes")
        nc.sync.dma_start(x_codes[:], x_words[0].rearrange("p c r -> p (c r)").bitcast(I32))
        w2_raw = load_first_weight(keep.tile([P, PACK, H], F32, name="w2_raw"), w2)
        gain = []
        for t in range(TILES):
            gain_t = reused.tile([P, 1], F32, name=f"gain{t}", offset=GAINS_AT + t * H)
            nc.sync.dma_start(gain_t[:], dealt_rows(gn, t))
            gain.append(gain_t)
        n1_sb = load_list("n1_sb", n1)
        n2_sb = load_list("n2_sb", n2)
        w3_raw = load_first_weight(reused.tile([P, PACK, H], F32, name="w3_raw", offset=W3_AT), w3)
        n4_sb = load_list("n4_sb", n4)
        n3_sb = load_list("n3_sb", n3)
        w4_raw = reused.tile([P, PACK, N], F32, name="w4_raw", offset=W4_AT)
        for j in range(PACK):
            nc.sync.dma_start(w4_raw[:, j, :], dealt_rows(w4, j))
        n5_sb = load_list("n5_sb", n5)
        n6_sb = load_list("n6_sb", n6)
        tab_sb = []
        for t in range(TILES):
            tab_t = keep.tile([P, J], F32, name=f"tab{t}")
            nc.sync.dma_start(tab_t[:], dealt_rows(tab, t))
            tab_sb.append(tab_t)

        def pick_words(name, lst):
            picked = keep.tile([P, S], U32, name=name, align_bytes=ALIGN)
            nc.vector.tensor_copy(picked[:], x_codes[:].bitcast(U32).indirect(lst[:]))
            return picked

        def pick_bytes(name, lst):
            picked = keep.tile([P, S], U8, name=name, align_bytes=ALIGN)
            nc.vector.tensor_copy(picked[:], x_bytes[:].indirect(lst[:]))
            return picked

        def group_weight(name, raw, tiles):
            grouped = keep.tile(
                [P, len(tiles), P * PACK], BF16, name="grouped", tag=f"{name}_grouped{tiles[0]}", align_bytes=ALIGN
            )
            for e, t in enumerate(tiles):
                nc.scalar.copy(
                    grouped[:, e, :].rearrange("p (b u i j) -> p b u j i", u=2, i=LINE, j=PACK),
                    raw[:].rearrange("p j (b t u i) -> p t b u j i", t=TILES, u=2, i=LINE)[:, t],
                )
            return grouped

        def quantise(name, grouped, scales):
            count = grouped.shape[1]
            codes = keep.tile([P, count * P], U32, name=f"{name}_codes", align_bytes=ALIGN)
            nc.vector.quantize_mx(
                out=codes[:].bitcast(FP8X4), scales=scales[:], in_=grouped[:].rearrange("p e c -> p (e c)")
            )
            return [(codes[:, e * P : (e + 1) * P], scales[:, e * P : (e + 1) * P]) for e in range(count)]

        def quantise_weight(name, raw, tiles):
            scales = keep.tile([P, len(tiles) * P], U8, name=f"{name}_scales{tiles[0]}", align_bytes=ALIGN)
            return quantise(f"{name}_{tiles[0]}", group_weight(name, raw, tiles), scales)

        def product(weight, codes, scales, width, bank):
            acc = psum.tile([P, S], F32, name="acc", tag=f"bank{bank}")
            nc.tensor.matmul_mx(
                out=acc[:, 0:width],
                lhsT=weight[0].bitcast(FP8X4),
                lhsT_scale=weight[1],
                rhs=codes[:].bitcast(FP8X4),
                rhs_scale=scales[:],
                start=True,
                stop=True,
            )
            return acc[:, 0:width]

        y_bytes = pick_bytes("y_bytes", offs_sb)
        d_bytes = pick_bytes("d_bytes", two_sb)
        b_bytes = pick_bytes("b_bytes", three_sb)
        w1_mx = [quantise_weight("w1", w1_raw, [t])[0] for t in range(TILES - 1)]
        y_words = pick_words("y_words", offs_sb)
        w1_last = group_weight("w1", w1_raw, [TILES - 1])
        d_words = pick_words("d_words", two_sb)
        b_words = pick_words("b_words", three_sb)

        m1, own, other = [], [], []

        def fetch_own(t, y_t):
            nc.scalar.activation(y_t[:], product(w1_mx[t], y_words, y_bytes, S, t), COPY, scale=gain[t][:])
            m1.append(y_t)
            own_t = keep.tile([P, W], F32, name=f"own{t}")
            nc.vector.tensor_scalar(own_t[:], y_t[:].indirect(n1_sb[:]), -0.5, 0.0, MULT, ADD)
            own.append(own_t)

        def fetch_other(t, d_t):
            nc.scalar.activation(d_t[:], product(w2_mx[t], d_words, d_bytes, S, TILES + t), COPY, scale=gain[t][:])
            other_t = keep.tile([P, W], F32, name=f"other{t}")
            nc.vector.tensor_copy(other_t[:], d_t[:].indirect(n2_sb[:]))
            other.append(other_t)

        def put_back(t):
            nc.vector.tensor_tensor(m1[t][:].indirect(n1_sb[:]), own[t][:], other[t][:], ADD)

        def over_gain(name, t):
            return reused.tile([P, H], U8, name=name, offset=GAINS_AT + t * H, align_bytes=ALIGN)

        for t in range(TILES - 1):
            fetch_own(t, keep.tile([P, S], F32, name=f"m1_{t}"))
        w2_mx = [quantise_weight("w2", w2_raw, [t])[0] for t in range(2)]
        w1_last_scales = keep.tile([P, P], U8, name="w1_last_scales", tag="w1_scales0", align_bytes=ALIGN)
        w1_mx.extend(quantise("w1_last", w1_last, w1_last_scales))
        fetch_own(3, keep.tile([P, S], F32, name="m1_3", tag="w2_grouped0", align_bytes=ALIGN))
        fetch_other(0, keep.tile([P, S], F32, name="d0"))
        put_back(0)
        w2_mx.extend(quantise_weight("w2", w2_raw, [2, 3]))
        fetch_other(1, keep.tile([P, S], F32, name="d1"))
        put_back(1)
        w3_grouped = group_weight("w3", w3_raw, range(TILES))
        fetch_other(2, reused.tile([P, S], F32, name="d2", offset=W3_AT + 2 * ROW_BYTES))
        w3_mx = quantise("w3", w3_grouped, over_gain("w3_scales", 2))
        put_back(2)
        w4_grouped = group_weight("w4", w4_raw, range(TILES))
        fetch_other(3, reused.tile([P, S], F32, name="d3", offset=W4_AT + 3 * ROW_BYTES))
        w4_mx = quantise("w4", w4_grouped, over_gain("w4_scales", 3))
        put_back(3)

        b = []
        gate = {}

        def fetch_gate(t, half, dst):
            nc.scalar.activation(dst, b[t][:].indirect(half_of(n4_sb, half)), SIGMOID)
            gate[t, half] = dst

        gate_early = keep.tile([P, 2 * TILES - 1, HALF], F32, name="gate_early")
        for t in range(TILES):
            b_t = reused.tile([P, S], F32, name=f"b{t}", offset=W4_AT + t * ROW_BYTES)
            nc.scalar.copy(b_t[:], product(w3_mx[t], b_words, b_bytes, S, t))
            b.append(b_t)
            fetch_gate(t, 0, gate_early[:, t, :])
        for t in range(TILES - 1):
            fetch_gate(t, 1, gate_early[:, TILES + t, :])

        h = [keep.tile([P, 2 * S], F32, name=f"h{t}") for t in range(TILES)]

        def apply_gate(dst, t, half):
            nc.vector.scalar_tensor_tensor(dst, m1[t][:, cols_of(half)], 2.0, gate[t, half], MULT, MULT)

        def make_z(dst, gated_t, t, half):
            nc.vector.tensor_tensor(dst, m1[t][:].indirect(half_of(n3_sb, half)), gated_t, SUBTRACT)

        def last_layer(z_half, half):
            z_grouped = keep.tile([P, HALF * PACK], BF16, name=f"z_grouped{half}", align_bytes=ALIGN)
            nc.scalar.activation(
                z_grouped[:].rearrange("p (c i t) -> p c t i", i=LINE, t=PACK),
                z_half[:].rearrange("p t (c i) -> p c t i", i=LINE),
                COPY,
                scale=-0.5,
            )
            z_codes = keep.tile([P, HALF], U32, name=f"z_codes{half}", align_bytes=ALIGN)
            z_scales = keep.tile([P, HALF], U8, name=f"z_scales{half}", align_bytes=ALIGN)
            nc.vector.quantize_mx(out=z_codes[:].bitcast(FP8X4), scales=z_scales[:], in_=z_grouped[:])
            for t in range(TILES):
                bank = TILES * (1 - half) + t
                nc.scalar.copy(h[t][:, cols_of(half)], product(w4_mx[t], z_codes, z_scales, HALF, bank))

        gated_a = keep.tile([P, TILES, HALF], F32, name="gated_a", tag="half_planes")
        z_a = keep.tile([P, TILES, HALF], F32, name="z_a")
        for t in range(TILES + 1):
            if t < TILES:
                apply_gate(gated_a[:, t, :], t, 0)
            if t > 0:
                make_z(z_a[:, t - 1, :], gated_a[:, t - 1, :], t - 1, 0)
        last_layer(z_a, 0)

        after_z_a = keep.tile([P, 3, HALF], F32, name="after_z_a", tag="z_a")
        fetch_gate(TILES - 1, 1, after_z_a[:, 2, :])
        z_b = keep.tile([P, TILES, HALF], F32, name="z_b", tag="half_planes")
        gated_b = keep.tile([P, 2, HALF], F32, name="gated_b")
        for pair, gated_pair in enumerate((gated_b, after_z_a)):
            for e in range(2):
                apply_gate(gated_pair[:, e, :], 2 * pair + e, 1)
            for e in range(2):
                make_z(z_b[:, 2 * pair + e, :], gated_pair[:, e, :], 2 * pair + e, 1)
        last_layer(z_b, 1)

        def add_kind(dst, t, half):
            nc.vector.tensor_tensor(dst, tab_sb[t][:].indirect(half_of(n5_sb, half)), h[t][:, cols_of(half)], ADD)

        def finish(first_t, second_t, t, half):
            res = keep.tile([P, HALF], F32, name=f"res{t}_{half}")
            nc.vector.tensor_tensor(res[:], first_t, second_t[:, cols_of(half)], MAX)
            nc.sync.dma_start(dealt_rows(out, t)[:, :, cols_of(half)], res[:])

        first_early = keep.tile([P, 2, HALF], F32, name="first_early")
        first_late = keep.tile([P, 2, HALF], F32, name="first_late", tag="half_planes")
        first_a = [pair[:, e, :] for pair in (first_early, first_late) for e in range(2)]
        for t in range(TILES):
            add_kind(first_a[t], t, 0)

        for t in range(TILES):
            second = keep.tile([P, S], F32, name=f"second{t}")
            nc.vector.tensor_copy(second[:], h[t][:].indirect(n6_sb[:]))
            first_b = keep.tile([P, HALF], F32, name=f"first_b{t}")
            add_kind(first_b[:], t, 1)
            finish(first_a[t], second, t, 0)
            finish(first_b[:], second, t, 1)
